import numpy as np
CORES = [0,24,48,72,96]
N = 5
ROOT = 2
def setup_inputs(rng):
    return {"x": rng.standard_normal((N, 128, 64), dtype=np.float32)}
def reference(x):
    y = np.full(x.shape, np.nan, x.dtype)
    y[ROOT] = x.sum(axis=0, dtype=np.float64).astype(x.dtype)
    return {"y": y}

@@ -1,0 +1,49 @@
+from concourse.bass import DstId, RemoteDMATransfer
+from concourse.mybir import AluOpType
+
+SCRATCH = {
+    "d": ("dram", [128, 64], "float32"),
+    "l0": ("dram", [128, 64], "float32"),
+    "l1": ("dram", [128, 64], "float32"),
+    "lb": ("dram", [128, 64], "float32"),
+}
+SEMAPHORES = ["ld", "sent", "a0", "a1", "ab"]
+
+ROOT = 48
+RELAY = 58
+OFF = 0x00FF
+NE = 8
+
+
+def rank_program(g, core, T, topo):
+    s = T.sem
+    plan = {
+        0: (ROOT, T.l0, s.a0),
+        96: (ROOT, T.l1, s.a1),
+        24: (RELAY, T.l0, s.a0),
+        72: (RELAY, T.l1, s.a0),
+    }
+    if core in plan:
+        dst, land, sem = plan[core]
+        rid, pid, _se = topo.addr(dst)
+        g.dma_start(T.d[:], T.x[:]).then_inc(s.ld, 16)
+        g.wait_ge(s.ld, 16)
+        g.remote_dma(land[:], T.d[:], sem, s.sent, pid, rid, OFF)
+        g.wait_ge(s.sent, NE)
+    elif core == RELAY:
+        rid, pid, _se = topo.addr(ROOT)
+        g.wait_ge(s.a0, 2 * NE)
+        g.remote_dma_fused(
+            [RemoteDMATransfer(dst_ids=[DstId(rid=rid, pnc=pid)], dma_engine_mask=OFF, remote_sem=s.ab,
+                               srcs=[T.l0[:], T.l1[:]], dsts=[T.lb[:]], alu_op=1)],
+            local_sem=s.sent)
+        g.wait_ge(s.sent, NE)
+    elif core == ROOT:
+        g.dma_start(T.y[:], T.x[:]).then_inc(s.ld, 16)
+        done = 16
+        for land, sem in ((T.l0, s.a0), (T.l1, s.a1), (T.lb, s.ab)):
+            g.wait_ge(sem, NE)
+            g.wait_ge(s.ld, done)
+            g.dma_start(T.y[:], land[:], accum_op=AluOpType.add, max_dma_last_dim=8192).then_inc(s.ld, 16)
+            done += 16
+        g.wait_ge(s.ld, done)

@@ -5,11 +5,13 @@ SCRATCH = {
     "d": ("dram", [128, 64], "float32"),
     "l0": ("dram", [128, 64], "float32"),
     "l1": ("dram", [128, 64], "float32"),
+    "la": ("dram", [128, 64], "float32"),
     "lb": ("dram", [128, 64], "float32"),
 }
-SEMAPHORES = ["ld", "sent", "a0", "a1", "ab"]
+SEMAPHORES = ["ld", "sent", "a0", "aa", "ab"]
 
 ROOT = 48
+HELP = 49
 RELAY = 58
 OFF = 0x00FF
 NE = 8
@@ -18,31 +20,32 @@ NE = 8
 def rank_program(g, core, T, topo):
     s = T.sem
     plan = {
-        0: (ROOT, T.l0, s.a0),
-        96: (ROOT, T.l1, s.a1),
-        24: (RELAY, T.l0, s.a0),
-        72: (RELAY, T.l1, s.a0),
+        0: (HELP, T.l0),
+        96: (HELP, T.l1),
+        24: (RELAY, T.l0),
+        72: (RELAY, T.l1),
     }
     if core in plan:
-        dst, land, sem = plan[core]
+        dst, land = plan[core]
         rid, pid, _se = topo.addr(dst)
         g.dma_start(T.d[:], T.x[:]).then_inc(s.ld, 16)
         g.wait_ge(s.ld, 16)
-        g.remote_dma(land[:], T.d[:], sem, s.sent, pid, rid, OFF)
+        g.remote_dma(land[:], T.d[:], s.a0, s.sent, pid, rid, OFF)
         g.wait_ge(s.sent, NE)
-    elif core == RELAY:
+    elif core in (RELAY, HELP):
         rid, pid, _se = topo.addr(ROOT)
+        m, n, land, sem = (OFF, 8, T.lb, s.ab) if core == RELAY else (0xFFFF, 16, T.la, s.aa)
         g.wait_ge(s.a0, 2 * NE)
         g.remote_dma_fused(
-            [RemoteDMATransfer(dst_ids=[DstId(rid=rid, pnc=pid)], dma_engine_mask=OFF, remote_sem=s.ab,
-                               srcs=[T.l0[:], T.l1[:]], dsts=[T.lb[:]], alu_op=1)],
+            [RemoteDMATransfer(dst_ids=[DstId(rid=rid, pnc=pid)], dma_engine_mask=m, remote_sem=sem,
+                               srcs=[T.l0[:], T.l1[:]], dsts=[land[:]], alu_op=1)],
             local_sem=s.sent)
-        g.wait_ge(s.sent, NE)
+        g.wait_ge(s.sent, n)
     elif core == ROOT:
         g.dma_start(T.y[:], T.x[:]).then_inc(s.ld, 16)
         done = 16
-        for land, sem in ((T.l0, s.a0), (T.l1, s.a1), (T.lb, s.ab)):
-            g.wait_ge(sem, NE)
+        for land, sem, n in ((T.la, s.aa, 16), (T.lb, s.ab, 8)):
+            g.wait_ge(sem, n)
             g.wait_ge(s.ld, done)
             g.dma_start(T.y[:], land[:], accum_op=AluOpType.add, max_dma_last_dim=8192).then_inc(s.ld, 16)
             done += 16

from concourse.bass import DstId, RemoteDMATransfer
from concourse.mybir import AluOpType

SCRATCH = {
    "d": ("dram", [128, 64], "float32"),
    "l0": ("dram", [128, 64], "float32"),
    "l1": ("dram", [128, 64], "float32"),
    "la": ("dram", [128, 64], "float32"),
    "lb": ("dram", [128, 64], "float32"),
}
SEMAPHORES = ["ld", "sent", "a0", "aa", "ab"]

ROOT = 48
HELP = 49
RELAY = 58
OFF = 0x00FF
NE = 8


def rank_program(g, core, T, topo):
    s = T.sem
    plan = {
        0: (HELP, T.l0),
        96: (HELP, T.l1),
        24: (RELAY, T.l0),
        72: (RELAY, T.l1),
    }
    if core in plan:
        dst, land = plan[core]
        rid, pid, _se = topo.addr(dst)
        g.dma_start(T.d[:], T.x[:]).then_inc(s.ld, 16)
        g.wait_ge(s.ld, 16)
        g.remote_dma(land[:], T.d[:], s.a0, s.sent, pid, rid, OFF)
        g.wait_ge(s.sent, NE)
    elif core in (RELAY, HELP):
        rid, pid, _se = topo.addr(ROOT)
        m, n, land, sem = (OFF, 8, T.lb, s.ab) if core == RELAY else (0xFFFF, 16, T.la, s.aa)
        g.wait_ge(s.a0, 2 * NE)
        g.remote_dma_fused(
            [RemoteDMATransfer(dst_ids=[DstId(rid=rid, pnc=pid)], dma_engine_mask=m, remote_sem=sem,
                               srcs=[T.l0[:], T.l1[:]], dsts=[land[:]], alu_op=1)],
            local_sem=s.sent)
        g.wait_ge(s.sent, n)
    elif core == ROOT:
        g.dma_start(T.y[:], T.x[:]).then_inc(s.ld, 16)
        done = 16
        for land, sem, n in ((T.la, s.aa, 16), (T.lb, s.ab, 8)):
            g.wait_ge(sem, n)
            g.wait_ge(s.ld, done)
            g.dma_start(T.y[:], land[:], accum_op=AluOpType.add, max_dma_last_dim=8192).then_inc(s.ld, 16)
            done += 16
        g.wait_ge(s.ld, done)
